import numpy as np, ml_dtypes
CORES = [2,3,42,43,82,83,122,123]
N = 8
BF = ml_dtypes.bfloat16
def gentries(a):
    return np.ascontiguousarray(a.reshape(8, 16, -1).transpose(0, 2, 1)).reshape(8, -1)
def gtable(e):
    e = np.asarray(e); return np.ascontiguousarray(e.reshape(8, -1, 16).transpose(0, 2, 1)).reshape(128, -1).astype(np.int32)
W, S, M, K, R, D = 2048, 2, 1024, 768, 4, 3
def places(rng):
    o = np.argsort(rng.random((N, 8, W)), axis=-1)[..., :2 * K]
    return np.array(o[..., :K]), np.array(o[..., K:])
def keys(rng):
    x = np.array(np.argsort(rng.random((N, 8, M)), axis=-1)[..., :K]).astype(np.int64)
    o = 2 * rng.integers(0, M // 2, (N, 8, 1)) + 1; e = rng.integers(0, M // 2, (N, 8, 1)); f = rng.integers(0, M // 2, (N, 8, 1))
    return (o + 2 * e * x + 2 * f * x * x) & (M - 1), x
def pack(m, th, A, B, a, b):
    return {"mk": np.ascontiguousarray(m.reshape(N, 128, W)).astype(np.float32).astype(BF), "th": np.ascontiguousarray(np.repeat(th, 16, axis=1).reshape(N, 128, 1)).astype(np.int32),
            "la": np.stack([gtable(v) for v in A]), "lb": np.stack([gtable(v) for v in B]), "ka": np.stack([gtable(v) for v in a]), "kb": np.stack([gtable(v) for v in b])}
def setup_inputs(rng):
    A, B = places(rng); a, b = keys(rng)
    return pack(rng.integers(0, 16, (N, 8, 16, W)), rng.integers(112, 160, (N, 8)), A, B, a, b)
def far(rng, back):
    G = max(g for g in range(1, W - 2 * K + 1) if g + max(0, (g - 1 + S // 2) // S - (M - K)) <= W - 2 * K)
    h = (G - 1 + S // 2) // S; mv = max(0, h - (M - K))
    x = int(rng.integers(1, K // 2))
    while ((W - 1 - S // 2 if back else 0) - (K - mv + x + G - 2)) % S: x += 1
    u = K - 1 - mv + x; base = u + G + K - x; e = u + G - 1; e = W - 1 - e if back else e; c = e // S
    near = c + np.arange(1, h + 1) * (1 if back else -1); rest = np.setdiff1d(np.arange(M), np.append(near, c))
    o = [rng.permutation(K) for q in range(N)]
    s = np.stack([np.concatenate([np.array([c]), rng.permutation(near)[:mv], rng.permutation(rest)[:K - 1 - mv]])[o[q]] for q in range(N)])
    A, B = np.zeros((N, K), np.int64), np.zeros((N, K), np.int64)
    for r in range(N):
        P = np.concatenate([np.array([u - 1]), base + 2 + 2 * np.arange(mv), rng.permutation(np.append(np.arange(x, u - 1), base))])
        Q = rng.permutation(np.concatenate([np.arange(x), u + G + np.arange(K - x)]))
        if back: A[r], B[r] = W - 1 - Q, W - 1 - P[o[(r - D) % N]]
        else: A[r], B[r] = P[o[r]], Q
    return A, B, s
def setup_inputs_full(rng):
    A, B = places(rng); a, b = keys(rng); th = np.full((N, 8), 241); lone = []
    for q in range(N):
        for g in range(6):
            k = (g + q) & 7; o = rng.permutation(2 * K)
            if k == 0:
                i = int(np.argmax(o)); o[i], o[K] = int(o[K]), int(o[i]); A[q, g], B[q, g] = o[:K], o[K:]
            elif k == 1:
                i = int(np.argmin(o)); o[i], o[0] = int(o[0]), int(o[i]); A[q, g], B[q, g] = W - 2 * K + o[:K], W - 2 * K + o[K:]
            elif k == 2:
                A[q, g] = rng.permutation(K); B[q, g] = W - K + rng.permutation(K)
            elif k == 3:
                A[q, g] = W - K + rng.permutation(K); B[q, g] = rng.permutation(K); j = int(rng.integers(0, 16))
                if q % 3 < 2: th[q, g] = 240; lone.append((q, g, K + j if q % 3 == 0 else W - 1 - K - j))
            elif k == 4:
                A[q, g] = S * rng.permutation(M)[:K]; B[q, g] = S * rng.permutation(M)[:K] + S // 2
            elif k == 5:
                A[q, g] = 2 * rng.permutation(K); B[q, g] = 2 * rng.permutation(K) + 1; th[q, g] = rng.integers(112, 160)
            else:
                p = 1 + rng.permutation(W - 2)[:2 * K]; A[q, g], B[q, g] = p[:K], p[K:]; i = rng.integers(0, K); j = rng.integers(0, K)
                A[q, g, i] = (W - 1, 0)[k - 6]; B[q, g, j] = (0, W - 1)[k - 6]
    for g in (6, 7):
        A[:, g], B[:, g], s = far(rng, g == 7)
        a[:, g] = 2 * rng.integers(0, M // 2, (N, 1)) + 1; b[:, g] = (s - 2 * a[:, g]) & (M - 1)
    m = rng.integers(0, 16, (N, 8, 16, W))
    m = np.where((rng.random((N, 8, 1, W)) < 0.25) & (th[:, :, None, None] == 241), 15, m)
    for q, g, w in lone: m[q, g, :, w] = 15
    return pack(m, th, A, B, a, b)
def setup_inputs_sites(rng):
    A, B = places(rng); a, b = keys(rng); th = np.tile(np.array([130, 1, 1, 1, 1, 240, 1, 1]), (N, 1)); t = np.arange(K)
    a[:, 0] = 1; b[:, 0] = t; a[:, 1] = M - 1; b[:, 1] = M - 1 - t
    a[:, 4] = 2 * rng.integers(0, M // 2, (N, 1)) + 1
    F = 1 << ((W - 1).bit_length() - 1); L = W - F
    f1 = rng.permutation(np.arange(-(-F // S), (F + L // 2 - 8) // S, 2))[:16]; f2 = rng.permutation(np.arange(L // 2 // S + 8, (L - 16) // S, 2))[:16]
    pl = np.concatenate([f1, f2]); n = len(pl); rest = np.setdiff1d(np.arange(M), pl); o4 = [rng.permutation(K) for q in range(N)]
    pa = np.concatenate([S * f1 - F, S * f2 - 1]); pb = np.concatenate([S * f1 + S // 2 + 1, S * f2 + S // 2 + F])
    other = np.setdiff1d(np.arange(W), np.concatenate([pa, pb, S * pl, S * pl + S // 2]))
    for q in range(N):
        b[q, 4] = (np.concatenate([pl, rng.permutation(rest)[:K - n]])[o4[q]] - 2 * a[q, 4]) & (M - 1)
        w = rng.permutation(other)
        A[q, 4] = np.concatenate([pa, w[:K - n]])[o4[q]]; B[q, 4] = np.concatenate([pb, w[K - n:2 * (K - n)]])[o4[(q - D) % N]]
    lim = 3 * (M - K) // 2; v = np.arange(M); v = v[(v % 3 == 1) | (v >= lim)]
    a[:, 5] = 3 * (2 * rng.integers(0, 4, (N, 1)) + 1); b[:, 5] = (np.stack([rng.permutation(v) for q in range(N)]) - 2 * a[:, 5]) & (M - 1)
    s = (a * 2 + b) & (M - 1); z = np.roll(s, D, axis=0)
    A[:, 2] = S * s[:, 2]; B[:, 2] = S * z[:, 2] + S // 2
    A[:, 3] = S * np.roll(s[:, 3], -1, axis=-1); B[:, 3] = S * np.roll(z[:, 3], -1, axis=-1) + S // 2
    s5, z5 = s[:, 5], z[:, 5]; go = (s5 % 3 == 1) & ((s5 < lim) | (S > 2)); kind = rng.integers(0, 3, (N, K))
    ga = (go & (kind != 2)).astype(np.int64); gb = np.roll(go & (kind != 1), D, axis=0).astype(np.int64)
    A[:, 5] = np.where(s5 % 3 == 2, S * s5 + S // 2, S * s5 - ga); B[:, 5] = np.where(z5 % 3 == 2, S * z5, S * z5 + S // 2 + gb)
    for q in range(N):
        for g in (6, 7):
            w = rng.random(W); w[S * s[q, g]] += 8 - g; w[S * z[q, g] + S // 2] += g - 5
            o = rng.permutation(np.argsort(w)[:2 * K]); A[q, g], B[q, g] = o[:K], o[K:]
    m = rng.integers(0, 16, (N, 8, 16, W)); m[:, 5] = np.where(taken(A, B)[:, 5][:, None, :], m[:, 5], 15)
    return pack(m, th, A, B, a, b)
def setup_inputs_spread(rng):
    A, B = places(rng); a, b = keys(rng)
    m = np.floor(rng.random((N, 8, 16, W)) * (rng.integers(0, 16, (N, 8, 1, W)) + 1)).astype(np.int64)
    return pack(m, rng.integers(1, 242, (N, 8)), A, B, a, b)
def setup_inputs_stall(rng):
    A, B = places(rng); a, b = keys(rng); th = np.full((N, 8), 1); th[((np.arange(N) // np.gcd(D, N)) & 1) == 1, 1::2] = 241
    m = rng.integers(0, 16, (N, 8, 16, W)) * (rng.random((N, 8, 1, W)) > 0.125)
    return pack(m, th, A, B, a, b)
def setup_inputs_ties(rng):
    A, B = places(rng); a, b = keys(rng); th = rng.integers(20, 220, (N, 8))
    T = th[:, :, None] + rng.choice(np.array([-2, -1, -1, -1, 0, 1]), (N, 8, W)); q = T // 16
    m = q[:, :, None, :] + (np.argsort(rng.random((N, 8, 16, W), dtype=np.float32), axis=2) < (T - 16 * q)[:, :, None, :])
    lo, hi = m[:, :, :8], m[:, :, 8:]; d = np.floor(rng.random(lo.shape) * (np.minimum(lo, 15 - hi) + 1)).astype(np.int64)
    return pack(np.concatenate([lo - d, hi + d], axis=2), th, A, B, a, b)
def check_inputs(d):
    bad = []
    x = d["mk"].astype(np.float32)
    if not np.all((x >= 0) & (x <= 15) & (x == np.floor(x))): bad.append("marks")
    for k, lo, hi in (("th", 1, 241), ("la", 0, W - 1), ("lb", 0, W - 1), ("ka", 1, M - 1), ("kb", 0, M - 1)):
        if np.min(d[k]) < lo or np.max(d[k]) > hi: bad.append("range of " + k)
    h = d["th"].reshape(N, 8, 16)
    if np.any(h != h[:, :, :1]): bad.append("th alike in a group")
    if np.any((d["ka"] & 1) == 0): bad.append("odd keys")
    A, B, a, b = [np.stack([gentries(v) for v in d[k]]).astype(np.int64) for k in ("la", "lb", "ka", "kb")]
    if np.any(np.diff(np.sort(np.concatenate([A, B], axis=2), axis=-1), axis=-1) == 0): bad.append("different places")
    for c in range(2, R + 1):
        if np.any(np.diff(np.sort((a * c + b) & (M - 1), axis=-1), axis=-1) == 0): bad.append("different sites in step " + str(c))
    return bad
def taken(A, B):
    o = np.zeros((N, 8, W), bool)
    np.put_along_axis(o, A, True, 2); np.put_along_axis(o, B, True, 2)
    return o
def reference(mk, th, la, lb, ka, kb):
    m = mk.astype(np.float32).astype(np.int64).reshape(N, 8, 16, W); t = th.astype(np.int64).reshape(N, 8, 16)[:, :, :1]
    A, B, a, b = [np.stack([gentries(v) for v in w]).astype(np.int64) for w in (la, lb, ka, kb)]
    at = np.arange(W); still = np.zeros((N, 8, K), bool)
    for c in range(1, R + 1):
        A0, B0 = A, B; held = taken(A, B)
        s = (a * c + b) & (M - 1); sa = S * s; sb = S * np.roll(s, D, axis=0) + S // 2
        A = np.where(still & ~np.take_along_axis(held, sa, 2), sa, A)
        B = np.where(np.roll(still, D, axis=0) & ~np.take_along_axis(held, sb, 2), sb, B)
        bar = np.add.reduce(m, axis=2) >= t
        up = np.maximum.accumulate(np.where(bar | taken(A, B), at + 1, 0), axis=2)
        up = np.concatenate([np.zeros((N, 8, 1), np.int64), up[..., :-1]], axis=2)
        A = np.take_along_axis(up, A, 2)
        dn = np.minimum.accumulate(np.where(bar | taken(A, B), at - 1, W - 1)[..., ::-1], axis=2)[..., ::-1]
        dn = np.concatenate([dn[..., 1:], np.full((N, 8, 1), W - 1)], axis=2)
        B = np.take_along_axis(dn, B, 2)
        ia, ib = A[:, :, None, :], B[:, :, None, :]
        va = np.take_along_axis(m, ia, 3); vb = np.take_along_axis(m, ib, 3)
        np.put_along_axis(m, ia, (va + np.roll(vb, -D, axis=0) + 1) & 15, 3)
        np.put_along_axis(m, ib, (vb + np.roll(va, D, axis=0) + 1) & 15, 3)
        still = (A == A0) & np.roll(B == B0, -D, axis=0)
    return {"ym": m.reshape(N, 128, W).astype(np.float32).astype(BF), "ya": np.stack([gtable(v) for v in A]).astype(np.float32), "yb": np.stack([gtable(v) for v in B]).astype(np.float32)}

from concourse.bass import DstId, RemoteDMATransfer
from concourse.mybir import AluOpType as OP, ActivationFunctionType as AF

W, K, NS, R, D = 2048, 768, 1024, 4, 3
KW = K // 16
KD = 40
YW = 16 + 2 * K
S = 2.0 ** -12
MAGIC = 3072.0

BF, F32, I32, U16, F16 = "bfloat16", "float32", "int32", "uint16", "float16"
SCRATCH = {}
for _w, _d, _l in (
        ("sbuf", BF, {"mk0": W, "M": W, "yg": W, "rr": W, "otab": W, "stab": W, "src": 2 * K, "U": W, "G1": 144, "G3": 144,
                      "ID": 128, "g9": 16, "oc": 96, "sg": 2 * K, "X": R * 2 * K, "Y": R * YW, "i128": 128, "wk": 256,
                      "occ": 128}),
        ("sbuf", F16, {"gat": 2 * K, "V": 128}),
        ("sbuf", I32, {"lab": 96, "kab": 96, "thi": 4, "ip": 4, "ipm": 4, "li": 128, "lj": 128, "pos": 192, "bq": 96,
                       "si": 144, "sj": 144}),
        ("sbuf", U16, {"idu": 128, "lu": 128, "colu": 96, "p1u": 96, "sLu": 144, "sRu": 144}),
        ("sbuf", F32, {"vtab": W, "thc": 4, "i130": 132, "pc": 8, "hs": 12, "cc": 12, "ec": 8, "ws": 128, "thr": 128,
                       "Cf": 128, "Cb": 128, "fr": 128, "gb": 128, "LX": 288, "T3": 96, "Yc": 64, "PP": 320, "mm": 128,
                       "EE": 256, "e2": 128, "dm": 256, "idf": 128, "t1": 96, "t2": 96, "so": 288, "sp": 288, "a1": 96,
                       "a2": 96, "a3": 96, "sL": 144, "sS": 144, "sR": 144, "yo": 96}),
        ("psum", F32, {"big": W, "ps": 512, "pd": 512, "pa": 512, "pb": 512})):
    for _n in _l:
        SCRATCH[_n] = (_w, [128, _l[_n]], _d)
SEMAPHORES = ["v", "a", "t", "g", "dl", "dk", "dt", "dm0", "dm1", "o0", "o1", "o2", "o3", "o4", "o5", "sent", "keys",
              "y1", "y2", "y3", "y4", "s1", "s2", "s3"]


def rank_program(g, core, T, topo):
    rank = T.rank_of(core)
    if rank is None:
        return
    n = len(T.cores)
    up, down = T.cores[(rank + D) % n], T.cores[(rank - D) % n]
    Q = {"v": g.vector, "a": g.scalar, "t": g.tensor, "g": g, "s": g.sync}
    count = {}
    known = {q: {} for q in Q}
    snap = {}
    writer, readers = {}, {}

    def need(q, ev):
        sem, val = ev
        if known[q].get(sem, 0) >= val:
            return
        Q[q].wait_ge(T.sem[sem], val)
        known[q][sem] = val
        for k, x in snap.get(ev, {}).items():
            if known[q].get(k, 0) < x:
                known[q][k] = x

    def op(q, fn, rd, wr, sem=None, inc=1):
        evs = []
        for k in rd:
            if k in writer:
                evs.append(writer[k])
            if k[0] == "#":
                evs += [e for e in readers.get(k, []) if e[0] != q]
        for k in wr:
            if k in writer:
                evs.append(writer[k])
            evs += readers.get(k, [])
        best = {}
        for s_, v_ in evs:
            if q == "t" and s_ == "t":
                continue
            best[s_] = max(best.get(s_, 0), v_)
        for s_, v_ in best.items():
            need(q, (s_, v_))
        sem = sem or q
        ins = fn()
        count[sem] = count.get(sem, 0) + inc
        ins.then_inc(T.sem[sem], inc)
        ev = (sem, count[sem])
        snap[ev] = dict(known[q])
        for k in rd:
            readers.setdefault(k, []).append(ev)
        for k in wr:
            writer[k] = ev
            readers[k] = []
        return ev

    V_, A_ = g.vector, g.scalar

    def ts(out, in0, s1, s2, o0, o1, rd, wr):
        if s2 is None:
            return op("v", lambda: V_.tensor_scalar(out, in0, s1, None, o0), rd, wr)
        return op("v", lambda: V_.tensor_scalar(out, in0, s1, s2, o0, o1), rd, wr)

    def tt(out, a, b, o, rd, wr):
        return op("v", lambda: V_.tensor_tensor(out, a, b, o), rd, wr)

    def cp(out, a, rd, wr):
        return op("v", lambda: V_.tensor_copy(out, a), rd, wr)

    def ms(out, c, wr):
        return op("v", lambda: V_.memset(out, c), [], wr)

    def scan(out, d0, d1, init, o0, o1, rd, wr):
        return op("v", lambda: V_.tensor_tensor_scan(out, d0, d1, init, o0, o1), rd, wr)

    def act(out, a, rd, wr, bias=None, scale=1.0):
        if bias is None:
            return op("a", lambda: A_.activation(out, a, AF.Copy, 0.0, scale), rd, wr)
        return op("a", lambda: A_.activation(out, a, AF.Identity, bias, scale), rd, wr)

    def mms(items, rd, wr):
        def fn():
            for it in items:
                ins = g.tensor.matmul(*it)
            return ins
        return op("t", fn, rd, wr)

    def iota(out, pat, base, cm, wr, flag=True):
        if flag:
            return op("g", lambda: g.iota(out, pat, base, cm, allow_small_or_imprecise_dtypes=True), [], wr)
        return op("g", lambda: g.iota(out, pat, base, cm), [], wr)

    def pick(out, in_, pat, o, base, cm, rd, wr):
        return op("g", lambda: g.affine_select(out, in_, pat, o, 0.0, base, cm), rd, wr)

    nsent = [0]

    def send(pairs, sem, rd):
        for k in rd:
            need("g", writer[k])
        tr = []
        for j, (dst, out, in_) in enumerate(pairs):
            e = topo.engines(core, dst)
            m = len(e) // len(pairs)
            rid, pid, _ = topo.addr(dst)
            tr.append(RemoteDMATransfer(dst_ids=[DstId(rid=rid, pnc=pid)],
                                        dma_engine_mask=sum(1 << x for x in e[j * m:(j + 1) * m]),
                                        remote_sem=T.sem[sem], src=in_, dst=out))
            nsent[0] += m
        g.remote_dma_fused(tr, local_sem=T.sem.sent)

    def arrivals(srcs, pairs):
        return sum(len(topo.engines(s_, core)) // pairs for s_ in srcs)

    G = lambda m, i: m[:, 15 - i:143 - i]
    bank = lambda q: T.big[:, 512 * q:512 * (q + 1)]
    blk = lambda m, q: m[:, 512 * q:512 * (q + 1)]
    wm1, wp1 = T.pa[:, 0:128], T.pa[:, 2:130]
    nf, bigr = T.pa[:, 132:260], T.pa[:, 260:388]
    H = W // 2

    op("s", lambda: g.sync.dma_start(T.lab[:, 0:KW], T.la[:]), [], [], "dl", 16)
    op("a", lambda: A_.dma_start(T.lab[:, KW:2 * KW], T.lb[:]), [], ["lab"], "dl", 16)
    op("a", lambda: A_.dma_start(T.mk0[:, 0:H], T.mk[:, 0:H]), [], ["mk0a"], "dm0", 16)
    op("s", lambda: g.sync.dma_start(T.mk0[:, H:W], T.mk[:, H:W]), [], ["mk0b"], "dm1", 16)
    op("s", lambda: g.sync.dma_start(T.kab[:, 0:KW], T.ka[:]), [], [], "dk", 16)
    op("s", lambda: g.sync.dma_start(T.kab[:, KW:2 * KW], T.kb[:]), [], ["kab"], "dk", 16)
    op("s", lambda: g.sync.dma_start(T.thi[:, 0:1], T.th[:], ), [], ["thi"], "dt", 16)

    iota(T.ip[:, 0:1], [[1, 1]], 0, 1, ["ip"], False)
    iota(T.i128[:], [[1, 128]], 0, 0, ["i128"])
    iota(T.hs[:, 0:6], [[-128, 6]], -16, 0, ["hs0"])
    iota(T.hs[:, 6:12], [[128, 6]], 16 + K, 0, ["hs1"])
    iota(T.i130[:, 0:130], [[1, 130]], -1, 0, ["i130"])
    iota(T.G1[:], [[0, 144]], 0, 0, ["G1"])
    iota(T.U[:], [[0, W]], 1, 0, ["U"])
    pick(T.ID[:], T.U[:, 0:128], [[-1, 128]], OP.is_equal, 0, 1, ["U"], ["ID"])
    pick(T.g9[:, 0:9], T.U[:, 0:9], [[-16, 9]], OP.is_ge, 0, 1, ["U"], ["g9"])
    pick(T.G1[:, 15::16], T.g9[:, 0:9], [[16, 9]], OP.is_ge, 15, -1, ["g9", "G1"], ["G1"])
    pick(T.U[:], T.U[:], [[-1, 16], [-16, 8], [0, 16]], OP.is_equal, 0, 1, ["U"], ["U"])

    ms(T.stab[:, 0:H], 0.0, ["stab0"])
    act(T.stab[:, H:W], T.stab[:, 0:H], ["stab0"], ["stab1"])
    ts(T.ipm[:, 0:1], T.ip[:, 0:1], 15, None, OP.bitwise_and, None, ["ip"], ["ipm0"])
    cp(T.pc[:, 0:1], T.ipm[:, 0:1], ["ipm0"], ["pc"])
    ts(T.ec[:, 0:3], T.i128[:, 0:3], T.pc[:, 0:1], None, OP.is_equal, None, ["i128", "pc"], ["ec"])
    ts(T.ec[:, 4:5], T.ec[:, 2:3], -0.5, None, OP.mult, None, ["ec"], ["ec2"])
    ts(T.ec[:, 3:4], T.ec[:, 1:2], -1.0, None, OP.mult, None, ["ec"], ["ec3"])
    ts(T.cc[:, 6:12], T.hs[:, 6:12], T.ec[:, 0:1], None, OP.mult, None, ["hs1", "ec"], ["cc1"])
    ts(T.cc[:, 0:6], T.hs[:, 0:6], T.ec[:, 0:1], T.ec[:, 4:5], OP.mult, OP.add, ["hs0", "ec", "ec2"], ["cc0"])
    for a in range(6, 10):
        ts(T.src[:, 128 * a:128 * (a + 1)], T.i128[:], T.ec[:, 1:2], T.cc[:, a:a + 1], OP.mult, OP.add,
           ["i128", "ec", "cc1"], ["src%d" % a])
    for a in range(6):
        ts(T.src[:, 128 * a:128 * (a + 1)], T.i128[:], T.ec[:, 3:4], T.cc[:, a:a + 1], OP.mult, OP.add,
           ["i128", "ec3", "cc0"], ["src%d" % a])
    for a in range(10, 12):
        act(T.src[:, 128 * a:128 * (a + 1)], T.i128[:], ["i128", "ec", "cc1"], ["src%d" % a],
            T.cc[:, a:a + 1], T.ec[:, 1:2])
    srck = ["src%d" % a for a in range(12)]
    cp(T.p1u[:], T.lab[:], ["lab"], ["p1u"])

    def scatter():
        op("v", lambda: V_.tensor_copy(T.stab[:, 0:W].indirect(T.p1u[:, 0:96]), T.src[:]),
           ["p1u"] + srck, ["stab0", "stab1"])

    scatter()
    act(T.pc[:, 6:7], T.pc[:, 0:1], ["pc"], ["pc6"], None, 128.0 * S)
    act(T.pc[:, 4:5], T.ec[:, 0:1], ["ec"], ["pc4"], T.ec[:, 2:3], 2.0 ** -24)
    act(T.wk[:, 0:128], T.i128[:], ["i128"], ["wk0"], None, S)
    act(T.pc[:, 5:6], T.ec[:, 1:2], ["ec", "pc4"], ["pc5"], T.pc[:, 4:5], 2.0 ** -24)
    act(T.wk[:, 128:256], T.i128[:], ["i128", "pc6"], ["wk1"], T.pc[:, 6:7], 0.0)
    act(T.ws[:], T.i130[:, 1:129], ["i130", "pc6"], ["ws"], T.pc[:, 6:7], S)
    for i in range(16):
        act(T.M[:, i::16], T.mk0[:, 128 * i:128 * (i + 1)], ["mk0a" if i < 8 else "mk0b"], ["Mi%d" % i])
    for q in range(4):
        writer["M%d" % q] = writer["Mi15"]
    act(T.G3[:], T.G1[:], ["G1", "pc5"], ["G3"], None, T.pc[:, 5:6])

    Mk = ["M0", "M1", "M2", "M3"]

    def fold_places():
        mms([(T.pd[:, 0:128], T.ID[:], T.wk[:, 0:128], True, False),
             (T.pd[:, 0:128], T.ID[:], T.wk[:, 128:256], False, False)], ["ID", "wk0", "wk1"], ["#pd"])

    def fold_ids():
        mms([(T.pd[:, 0:128], G(T.G3, i), T.stab[:, 128 * i:128 * (i + 1)], False, i == 15) for i in range(16)],
            ["G3", "stab0", "stab1"], ["#pd"])

    def fold_marks(last):
        mms([(T.ps[:, 0:128], G(T.G1, i), T.M[:, i::16], i == 0, last and i == 15) for i in range(16)],
            ["G1"] + Mk, ["#ps"])

    def fold_half(m, key, h, last):
        mms([(T.ps[:, 64 * h:64 * (h + 1)], G(T.G1, i), m[:, H * h + i:H * (h + 1):16], False,
              last and i == 15) for i in range(16)], ["G1", key + str(2 * h), key + str(2 * h + 1)], ["#ps"])

    fold_marks(True)
    fold_places()
    fold_ids()
    act(T.stab[:], T.M[:], Mk, ["stab0", "stab1"], None, 0.0)
    for c in range(2, R + 1):
        ts(T.si[:, KW * (c - 2):KW * (c - 1)], T.kab[:, 0:KW], float(c), None, OP.mult, None, ["kab"], ["si%d" % c])
    ts(T.pa[:, 0:130], T.i130[:, 0:130], S, T.pc[:, 6:7], OP.mult, OP.add, ["i130", "pc6"], ["#wc"])
    for c in range(2, R + 1):
        tt(T.sj[:, KW * (c - 2):KW * (c - 1)], T.si[:, KW * (c - 2):KW * (c - 1)], T.kab[:, KW:2 * KW], OP.add,
           ["kab", "si%d" % c], ["sj%d" % c])
    cp(T.thc[:, 0:1], T.thi[:, 0:1], ["thi"], ["thc0"])
    ts(T.si[:], T.sj[:], NS - 1, None, OP.bitwise_and, None, ["sj2", "sj3", "sj4"], ["si2", "si3", "si4"])
    ts(T.thc[:, 1:2], T.thi[:, 0:1], -16.0 * MAGIC, None, OP.add, None, ["thi"], ["thc1"])
    ts(T.sS[:], T.si[:], 2.0, 1.0, OP.mult, OP.add, ["si2"], ["sS"])
    send([(up, T.sR[:], T.sS[:])], "keys", ["sS"])
    writer["sR"] = ("keys", arrivals([down], 1))
    ms(T.LX[:, 128:160], 0.0, ["LXF"])
    ms(T.Yc[:, 0:32:16], -S, ["Yc0"])
    ms(T.Yc[:, 47:64:16], W * S, ["Yc1"])

    def prepare(c):
        p0 = T.pd[:, 0:128]
        tt(T.gb[:], p0, T.ws[:], OP.not_equal, ["#pd", "ws"], ["gb"])
        tt(T.Cf[:], p0, T.ws[:], OP.max, ["#pd", "ws"], ["Cf"])
        ts(T.thr[:], T.gb[:], -1.0e6, T.thc[:, min(c - 1, 1):min(c - 1, 1) + 1], OP.mult, OP.add,
           ["gb", "thc0", "thc1"], ["thr"])
        tt(T.Cb[:], p0, T.ws[:], OP.min, ["#pd", "ws"], ["Cb"])
        ts(bigr, p0, 0.0, 0.25, OP.is_ge, OP.subtract, ["#pd"], ["#bigr"])

    prepare(1)

    for c in range(1, R + 1):
        last = c == R
        sm = T.ps[:, 0:128]
        tt(nf, sm, T.thr[:], OP.is_ge, ["#ps", "thr"], ["#nf"])
        tt(T.fr[:], sm, T.thr[:], OP.is_lt, ["#ps", "thr"], ["fr"])
        scan(T.LX[:, 0:128], nf, T.Cf[:], -S, OP.add, OP.min, ["#nf", "Cf"], ["LXf"])
        tt(T.gb[:], nf, T.Cb[:], OP.mult, ["#nf", "Cb"], ["gb"])
        ts(T.LX[:, 128:129], T.LX[:, 127:128], -S, None, OP.is_equal, None, ["LXf"], ["LXF"])
        scan(T.LX[:, 287:159:-1], T.fr[:, ::-1], T.gb[:, ::-1], 0.0, OP.mult, OP.add, ["fr", "gb"], ["LXb"])
        op("v", lambda: V_.transpose(T.T3[:], T.LX[:, 96:192]), ["LXf", "LXF", "LXb"], ["T3"])
        for h in (0, 16):
            scan(T.Yc[:, h + 1:h + 16], T.T3[:, h:h + 15], T.T3[:, h:h + 15], -S, OP.max, OP.max,
                 ["T3"], ["Ycf%d" % h])
        for h in (0, 16):
            scan(T.Yc[:, 46 + h:31 + h:-1], T.T3[:, 47 + h:32 + h:-1], T.T3[:, 79 + h:64 + h:-1], W * S,
                 OP.mult, OP.add, ["T3"], ["Ycb%d" % h])
        op("v", lambda: V_.transpose(T.PP[:, 0:32], T.Yc[:, 0:32]), ["Yc0", "Ycf0", "Ycf16"], ["cf"])
        op("v", lambda: V_.transpose(T.PP[:, 288:320], T.Yc[:, 32:64]), ["Yc1", "Ycb0", "Ycb16"], ["cb"])
        scan(T.PP[:, 32:160], nf, T.Cf[:], T.PP[:, 31:32], OP.add, OP.min, ["#nf", "Cf", "cf"], ["Pf"])
        scan(T.PP[:, 287:159:-1], T.fr[:, ::-1], T.gb[:, ::-1], T.PP[:, 288:289], OP.mult, OP.add,
             ["fr", "gb", "cb"], ["Pb"])
        E, Ib, Bx = T.PP[:, 31:159], T.PP[:, 160:288], T.PP[:, 161:289]
        tt(bigr, E, bigr, OP.max, ["Pf", "cf", "#bigr"], ["#bigr"])
        tt(T.mm[:], Bx, wp1, OP.max, ["Pb", "cb", "#wc"], ["mm"])
        xb, yb = 2 * K * (c - 1), YW * (c - 1)

        def unfold(m, key):
            for q in range(4):
                mms([(T.big[:, 128 * i:128 * (i + 1)], T.U[:, 128 * i:128 * (i + 1)], m[:], True, True)
                     for i in range(4 * q, 4 * q + 4)], ["U", key], ["#b%d" % q])

        def send_columns(m, keys):
            ts(T.X[:, xb:xb + K], m[:, 0:W].indirect(T.colu[:, 0:KW]), 1.0, None, OP.add, None,
               keys + ["colu"], ["XA"])
            act(T.X[:, xb + K:xb + 2 * K], m[:, 0:W].indirect(T.colu[:, KW:2 * KW]), keys + ["colu"], ["XB"], 1.0)
            send([(up, T.Y[:, yb + 16 + K:yb + YW], T.X[:, xb:xb + K]),
                  (down, T.Y[:, yb + 16:yb + 16 + K], T.X[:, xb + K:xb + 2 * K])], "y%d" % c, ["XA", "XB"])
            writer["Y"] = ("y%d" % c, arrivals([up, down], 2))

        def open_sums():
            for q in range(4):
                mms([(bank(q), T.ID[:], blk(T.M, q), True, False)], ["ID", "M%d" % q], ["#b%d" % q])
                if last:
                    mms([(bank(q), T.ID[:], T.sg[:, 0:512], False, False)], ["ID", "sgA"], ["#b%d" % q])

        if last:
            ts(T.pb[:, 0:128], bigr, 1 / S, 0.8, OP.mult, OP.add, ["#bigr"], ["#rnd"])
            ts(T.e2[:], T.mm[:], 1 / S, -1.2, OP.mult, OP.add, ["mm"], ["e2"])
            tt(T.li[:], T.pb[:, 0:128], T.e2[:], OP.min, ["#rnd", "e2"], ["li"])
            ts(T.lj[:], T.li[:], 7, None, OP.logical_shift_right, None, ["li"], ["lj"])
            ts(T.pb[:, 256:384], T.lj[:], -2047.0 / 16, None, OP.mult, None, ["lj"], ["#dd"])
            tt(T.dm[:, 0:128], T.pb[:, 256:384], T.li[:], OP.add, ["#dd", "li"], ["dm"])
            ts(T.lu[:], T.dm[:, 0:128], 16.0, None, OP.mult, None, ["dm"], ["lu"])
            act(T.yg[:, H:W], T.M[:, 0:W].indirect(T.lu[:, 64:128]), Mk + ["lu"], ["yg2", "yg3"])
            cp(T.yg[:, 0:H], T.M[:, 0:W].indirect(T.lu[:, 0:64]), Mk + ["lu"], ["yg0", "yg1"])
            send_columns(T.yg, ["yg0", "yg1", "yg2", "yg3"])
        tt(T.V[:], bigr, T.mm[:], OP.min, ["#bigr", "mm"], ["V"])
        unfold(T.V, "V")
        for q in range(3):
            act(blk(T.vtab, q), bank(q), ["#b%d" % q], ["vt%d" % q])
        ts(T.pb[:, 0:256], T.PP[:, 32:288], MAGIC, MAGIC, OP.add, OP.subtract, ["Pf", "Pb"], ["#rnd"])
        tt(T.e2[:], T.mm[:], wp1, OP.is_equal, ["mm", "#wc"], ["e2"])
        ts(nf, Ib, 0.0, None, OP.is_ge, None, ["Pb"], ["#nf"])
        tt(T.EE[:, 128:256], E, wm1, OP.is_ge, ["Pf", "cf", "#wc"], ["EE1"])
        tt(T.pb[:, 256:512], T.PP[:, 32:288], T.pb[:, 0:256], OP.subtract, ["Pf", "Pb", "#rnd"], ["#dd"])
        cp(blk(T.vtab, 3), bank(3), ["#b3"], ["vt3"])
        tt(T.EE[:, 0:128], T.e2[:], nf, OP.mult, ["e2", "#nf"], ["EE0"])
        tt(T.dm[:, 128:256], T.EE[:, 128:256], T.pb[:, 384:512], OP.mult, ["EE1", "#dd"], ["dm"])
        if c == 1:
            ms(T.oc[:, 0:KW], 16 * S, ["oc0"])
            ms(T.oc[:, KW:96], -16 * S, ["oc1"])
        tt(T.pb[:, 0:128], T.EE[:, 0:128], T.pb[:, 256:384], OP.mult, ["EE0", "#dd"], ["#rnd"])
        tt(T.idf[:], T.pb[:, 0:128], T.dm[:, 128:256], OP.subtract, ["#rnd", "dm"], ["idf"])
        if not last:
            ts(T.occ[:], T.idf[:], 0.0, 1.0 / 16, OP.is_equal, OP.mult, ["idf"], ["occ"])
        else:
            ts(T.idu[:], T.idf[:], 2.0 ** 24, None, OP.mult, None, ["idf"], ["idu"])
            ms(T.sg[:, 0:512], MAGIC, ["sgA"])
            open_sums()
        vk = ["vt0", "vt1", "vt2", "vt3"]
        cp(T.gat[:, 0:16 * KD], T.vtab[:, 0:W].indirect(T.p1u[:, 0:KD]), vk + ["p1u"], ["gatA"])
        act(T.gat[:, 16 * KD:2 * K], T.vtab[:, 0:W].indirect(T.p1u[:, KD:2 * KW]), vk + ["p1u"], ["gatB"])
        if not last:
            unfold(T.occ, "occ")
        dg = T.pd[:, 128:224]
        mms([(dg, T.ID[:], T.oc[:], True, False)], ["ID", "oc0", "oc1"], ["#pd"])
        mms([(dg, G(T.G1, i), T.gat[:, i::16], False, i == 15) for i in range(16)], ["G1", "gatA", "gatB"], ["#pd"])
        if not last:
            ts(T.idu[:], T.idf[:], 2.0 ** 24, None, OP.mult, None, ["idf"], ["idu"])
            for q in range(3):
                act(blk(T.otab, q), bank(q), ["#b%d" % q], ["ot%d" % q])
            cp(blk(T.otab, 3), bank(3), ["#b3"], ["ot3"])
        if c == 1:
            ts(T.sLu[:], T.si[:], 2.0, None, OP.mult, None, ["si2"], ["sLu"])
        o = 96 * (c % 2)
        new = T.pos[:, o:o + 96]
        old = T.lab[:] if c == 1 else T.pos[:, 96 - o:192 - o]
        kn, ko = "pos%d" % (c % 2), "lab" if c == 1 else "pos%d" % (1 - c % 2)

        def columns(p, key):
            ts(T.t1[:], T.bq[:], -2047.0 / 16, None, OP.mult, None, ["bq"], ["t1"])
            if key == kn:
                tt(so, new, old, OP.is_equal, [kn, ko], ["so%d" % c])
                send([(up, T.sp[:, b + KW:b + 96], T.so[:, b:b + KW]),
                      (down, T.sp[:, b:b + KW], T.so[:, b + KW:b + 96])], "s%d" % c, ["so%d" % c])
                writer["sp%d" % c] = ("s%d" % c, arrivals([up, down], 2))
            tt(T.t2[:], T.t1[:], p, OP.add, ["t1", key], ["t2"])
            ts(T.colu[:], T.t2[:], 16.0, None, OP.mult, None, ["t2"], ["colu"])

        def ygather(eng, q):
            win = T.Y[:, yb:yb + YW].indirect(T.idu[:, 32 * q:32 * (q + 1)])
            (act if eng == "a" else cp)(blk(T.yg, q), win, ["Y", "Yz%d" % (c - 1), "idu"], ["yg%d" % q])
            mms([(bank(q), T.ID[:], blk(T.yg, q), False, True)], ["ID", "yg%d" % q], ["#b%d" % q])

        def carry(eng, q, bias):
            if eng == "a":
                act(blk(T.rr, q), bank(q), ["#b%d" % q], ["rr%d" % q], bias, -1.0)
            else:
                ts(blk(T.rr, q), bank(q), -1.0, bias, OP.mult, OP.add, ["#b%d" % q], ["rr%d" % q])

        if not last:
            b = 96 * (c - 1)
            so = T.so[:, b:b + 96]
            ts(T.bq[:], dg, 2.0, -0.2 / 128 - 0.498, OP.mult, OP.add, ["#pd"], ["bq"])
            ts(new, dg, 256.0, -0.2, OP.mult, OP.add, ["#pd"], [kn])
            columns(new, kn)
            send_columns(T.M, Mk)
            open_sums()
            fold_marks(False)
            ok = ["ot0", "ot1", "ot2", "ot3"]
            sb = KW * (c - 1)
            if c == 1:
                cp(T.sRu[:], T.sR[:], ["sR"], ["sRu"])
            cp(T.sg[:, 0:K], T.otab[:, 0:W].indirect(T.sLu[:, sb:sb + KW]), ok + ["sLu"], ["sgA"])
            act(T.sg[:, K:2 * K], T.otab[:, 0:W].indirect(T.sRu[:, sb:sb + KW]), ok + ["sRu"], ["sgB"])
            mms([(dg, G(T.G1, i), T.sg[:, i::16], i == 0, i == 15) for i in range(16)], ["G1", "sgA", "sgB"], ["#pd"])
            if c == 1:
                ts(T.sL[:], T.si[:], 2.0, None, OP.mult, None, ["si2"], ["sL"])
                for k in range(R):
                    ms(T.Y[:, YW * k:YW * k + 16], 0.0, ["Yz%d" % k])
            tt(T.a1[:, KW:96], T.sR[:, sb:sb + KW], T.pos[:, o + KW:o + 96], OP.subtract, ["sR", kn], ["a1b"])
            tt(T.a1[:, 0:KW], T.sL[:, sb:sb + KW], T.pos[:, o:o + KW], OP.subtract, ["sL", kn], ["a1"])
            tt(T.pb[:, 0:96], so, T.sp[:, b:b + 96], OP.mult, ["so%d" % c, "sp%d" % c], ["#rnd"])
            tt(T.a2[:], T.a1[:], T.pb[:, 0:96], OP.mult, ["a1", "a1b", "#rnd"], ["a2"])
            tt(T.pb[:, 256:352], T.a2[:], dg, OP.mult, ["a2", "#pd"], ["#dd"])
            tt(T.a3[:], T.pb[:, 256:352], new, OP.add, ["#dd", kn], ["a3"])
            cp(T.p1u[:], T.a3[:], ["a3"], ["p1u"])
            scatter()
            fold_places()
            for h in (0, 1):
                for q in (2 * h, 2 * h + 1):
                    ygather("a", q)
                fold_half(T.yg, "yg", h, False)
            fold_ids()
            if c < R - 1:
                iota(T.stab[:], [[0, W]], 0, 0, ["stab0", "stab1"])
            for q in range(4):
                carry("vvaa"[q], q, 7.5 - MAGIC)
            fold_half(T.rr, "rr", 1, False)
            fold_half(T.rr, "rr", 0, True)
            prepare(c + 1)
            if c == R - 1:
                ts(T.bq[:], T.a3[:], 1.0 / 128, -0.498, OP.mult, OP.add, ["a3"], ["bq"])
                columns(T.a3[:], "a3")
            for q in range(4):
                act(blk(T.M, q), bank(q), ["#b%d" % q], ["M%d" % q])
        else:
            ts(new, dg, 256.0, -0.2, OP.mult, OP.add, ["#pd"], [kn])
            cp(T.yo[:], new, [kn], ["yo"])
            op("s", lambda: g.sync.dma_start(T.ya[:], T.yo[:, 0:KW]), ["yo"], ["ya"], "o0", 16)
            op("s", lambda: g.sync.dma_start(T.yb[:], T.yo[:, KW:96]), ["yo"], ["yb"], "o1", 16)
            for q in range(4):
                ygather("va"[q % 2], q)
            for q in range(4):
                carry("vaaa"[q], q, 7.5)
            for h in (0, 1):
                for i in range(16):
                    tt(T.mk0[:, 128 * i + 64 * h:128 * i + 64 * h + 64], T.big[:, H * h + i:H * (h + 1):16],
                       T.rr[:, H * h + i:H * (h + 1):16], OP.add,
                       ["#b%d" % (2 * h), "#b%d" % (2 * h + 1), "rr%d" % (2 * h), "rr%d" % (2 * h + 1)], ["z%d" % i])
                    if h and i % 4 == 3:
                        q = i // 4
                        op("s", lambda q=q: g.sync.dma_start(blk(T.ym, q), blk(T.mk0, q)),
                           ["z%d" % i], ["ym%d" % q], "o%d" % (2 + q), 16)

    for s_ in ("o0", "o1", "o2", "o3", "o4", "o5", "v", "a", "t", "g"):
        need("s", (s_, count[s_]))
    g.wait_ge(T.sem.sent, nsent[0])
